import numpy as np, ml_dtypes
CORES = [23,119,17,113]
N = 4
C = 64
def setup_inputs(rng):
    x = rng.standard_normal((N, 128, C), dtype=np.float32) * (0.25 + np.abs(rng.standard_normal((N, 1, C), dtype=np.float32)))
    return {"x": x.astype(ml_dtypes.bfloat16)}
def setup_inputs_big(rng):
    d = setup_inputs(rng)
    for k in ("x",): d[k] = (d[k].astype(np.float32) * 1048576.0).astype(d[k].dtype)
    return d
def setup_inputs_small(rng):
    d = setup_inputs(rng)
    for k in ("x",): d[k] = (d[k].astype(np.float32) * (1 / 1048576.0)).astype(d[k].dtype)
    return d
def setup_inputs_apart(rng):
    d = setup_inputs(rng)
    f = (10.0 ** rng.permutation(np.linspace(-1.5, 1.5, N))).astype(np.float32).reshape(N, 1, 1)
    for k in ("x",): d[k] = (d[k].astype(np.float32) * f).astype(d[k].dtype)
    return d
def setup_inputs_mixed(rng):
    d = setup_inputs(rng)
    f = (10.0 ** rng.uniform(-3, 3, (N, 1, C))).astype(np.float32); shape = rng.integers(3, size=(N, 1, C))
    for k in ("x",):
        x = d[k].astype(np.float32)
        m = x.mean(axis=1, keepdims=True); level = m + np.sign(x - m) * np.abs(x - m).mean(axis=1, keepdims=True) * rng.uniform(0.9, 1.1, x.shape).astype(np.float32)
        other = x * np.where(rng.random(x.shape) < 0.016, 100.0, 1.0).astype(np.float32)
        d[k] = (np.where(shape == 1, level, np.where(shape == 2, other, x)) * f).astype(d[k].dtype)
    return d
def reference(x):
    X = x.astype(np.float64); U = X / np.sqrt((X ** 2).sum(axis=1, keepdims=True))
    y = np.full((N, C, N * C), np.nan)
    for r in range(N):
        for s in range(N):
            if s != r: y[r][:, C * s:C * s + C] = U[r].T @ U[s]
    return {"y": y.astype(ml_dtypes.bfloat16)}

@@ -1,0 +1,122 @@
+from concourse.bass import DstId, RemoteDMATransfer
+from concourse.mybir import AluOpType, ActivationFunctionType
+
+C = 64
+HALF = 96
+ENG = 4
+
+SCRATCH = {
+    "xs": ("sbuf", [128, C], "bfloat16"),
+    "xo": ("sbuf", [128, 3 * C], "bfloat16"),
+    "ones": ("sbuf", [128, 128], "bfloat16"),
+    "sqs": ("sbuf", [128, C], "bfloat16"),
+    "sqo": ("sbuf", [128, 3 * C], "bfloat16"),
+    "ninv": ("sbuf", [128, C], "float32"),
+    "us": ("sbuf", [128, C], "bfloat16"),
+    "oinv": ("sbuf", [128, HALF], "float32"),
+    "ysb": ("sbuf", [128, HALF], "bfloat16"),
+    "ps_own": ("psum", [128, 512], "float32"),
+    "ps_ss": ("psum", [128, 512], "float32"),
+    "ps_g": ("psum", [128, 512], "float32"),
+}
+SEMAPHORES = ["loaded", "sent", "arr", "c_ones", "s_sq", "t_own", "s_rt", "v_inv", "v_u",
+              "sq_o", "t_ss", "t_g", "s_rto", "v_oinv", "v_y", "stored"]
+
+
+def _engines(allowed, used, n):
+    m = 0
+    for b in range(16):
+        if n and (allowed >> b) & 1 and not (used >> b) & 1:
+            m |= 1 << b
+            n -= 1
+    return m
+
+
+def _segments(others):
+    segs = []
+    for h in range(2):
+        c = HALF * h
+        while c < HALF * (h + 1):
+            e = min(HALF * (h + 1), (c // C + 1) * C)
+            y0 = others[c // C] * C + c % C
+            if segs and segs[-1][0] == h and segs[-1][4] == y0:
+                segs[-1][2] = e - HALF * h
+                segs[-1][4] = y0 + e - c
+            else:
+                segs.append([h, c - HALF * h, e - HALF * h, y0, y0 + e - c])
+            c = e
+    return segs
+
+
+def rank_program(g, core, T, topo):
+    rank = T.rank_of(core)
+    if rank is None:
+        return
+    sem = T.sem
+    A = ActivationFunctionType
+    n = len(T.cores)
+    others = [s for s in range(n) if s != rank]
+    tens, vec, sca, syn = g.tensor, g.vector, g.scalar, g.sync
+
+    syn.dma_start(T.xs[:], T.x[:]).then_inc(sem.loaded, 16)
+    vec.memset(T.ones[:], 1.0).then_inc(sem.c_ones, 1)
+
+    transfers = []
+    used = 0
+    for s in sorted(others, key=lambda s: topo.mask(core, T.cores[s])):
+        dst = T.cores[s]
+        m = _engines(topo.mask(core, dst), used, ENG)
+        used |= m
+        rid, pid, _ = topo.addr(dst)
+        slot = rank if rank < s else rank - 1
+        transfers.append(RemoteDMATransfer(dst_ids=[DstId(rid=rid, pnc=pid)], dma_engine_mask=m, remote_sem=sem.arr,
+                                           src=T.xs[:], dst=T.xo[:, slot * C:(slot + 1) * C]))
+    g.wait_ge(sem.loaded, 16)
+    g.remote_dma_fused(transfers, local_sem=sem.sent)
+    landed = ENG * len(others)
+
+    sca.wait_ge(sem.loaded, 16)
+    sca.activation(T.sqs[:], T.xs[:], A.Square).then_inc(sem.s_sq, 1)
+    tens.wait_ge(sem.c_ones, 1)
+    tens.wait_ge(sem.s_sq, 1)
+    tens.matmul(T.ps_own[:, 0:C], T.ones[:], T.sqs[:], True, True).then_inc(sem.t_own, 1)
+    sca.wait_ge(sem.t_own, 1)
+    sca.activation(T.ninv[:], T.ps_own[:, 0:C], A.Sqrt).then_inc(sem.s_rt, 1)
+    vec.wait_ge(sem.s_rt, 1)
+    vec.reciprocal(T.ninv[:], T.ninv[:]).then_inc(sem.v_inv, 1)
+    vec.wait_ge(sem.v_inv, 1)
+    vec.wait_ge(sem.loaded, 16)
+    vec.tensor_tensor(T.us[:], T.xs[:], T.ninv[:], AluOpType.mult).then_inc(sem.v_u, 1)
+
+    sca.wait_ge(sem.arr, landed)
+    sca.activation(T.sqo[:, 0:2 * C], T.xo[:, 0:2 * C], A.Square).then_inc(sem.sq_o, 1)
+    vec.wait_ge(sem.arr, landed)
+    vec.tensor_tensor(T.sqo[:, 2 * C:3 * C], T.xo[:, 2 * C:3 * C], T.xo[:, 2 * C:3 * C],
+                      AluOpType.mult).then_inc(sem.sq_o, 1)
+
+    tens.wait_ge(sem.sq_o, 2)
+    for h in range(2):
+        tens.matmul(T.ps_ss[C * h:C * (h + 1), 0:HALF], T.ones[:, 0:C], T.sqo[:, HALF * h:HALF * (h + 1)],
+                    True, True).then_inc(sem.t_ss, 1)
+    tens.wait_ge(sem.v_u, 1)
+    tens.wait_ge(sem.arr, landed)
+    for h in range(2):
+        tens.matmul(T.ps_g[C * h:C * (h + 1), 0:HALF], T.us[:], T.xo[:, HALF * h:HALF * (h + 1)],
+                    True, True).then_inc(sem.t_g, 1)
+
+    sca.wait_ge(sem.t_ss, 2)
+    sca.activation(T.oinv[:], T.ps_ss[:, 0:HALF], A.Sqrt).then_inc(sem.s_rto, 1)
+    vec.wait_ge(sem.s_rto, 1)
+    vec.reciprocal(T.oinv[:], T.oinv[:]).then_inc(sem.v_oinv, 1)
+    vec.wait_ge(sem.v_oinv, 1)
+    vec.wait_ge(sem.t_g, 2)
+    vec.tensor_tensor(T.ysb[:], T.ps_g[:, 0:HALF], T.oinv[:], AluOpType.mult).then_inc(sem.v_y, 1)
+
+    segs = _segments(others)
+    syn.wait_ge(sem.v_y, 1)
+    sca.wait_ge(sem.v_y, 1)
+    for k, (h, c0, c1, y0, y1) in enumerate(segs):
+        q = syn if k % 2 == 0 else sca
+        q.dma_start(T.y[:, y0:y1], T.ysb[C * h:C * (h + 1), c0:c1]).then_inc(sem.stored, 16)
+    syn.wait_ge(sem.stored, 16 * len(segs))
+    g.wait_ge(sem.sent, landed)

@@ -2,25 +2,25 @@ from concourse.bass import DstId, RemoteDMATransfer
 from concourse.mybir import AluOpType, ActivationFunctionType
 
 C = 64
-HALF = 96
 ENG = 4
 
 SCRATCH = {
     "xs": ("sbuf", [128, C], "bfloat16"),
     "xo": ("sbuf", [128, 3 * C], "bfloat16"),
+    "ro": ("sbuf", [128, 3 * C], "bfloat16"),
     "ones": ("sbuf", [128, 128], "bfloat16"),
     "sqs": ("sbuf", [128, C], "bfloat16"),
-    "sqo": ("sbuf", [128, 3 * C], "bfloat16"),
+    "rf": ("sbuf", [128, C], "float32"),
+    "rs": ("sbuf", [128, C], "bfloat16"),
     "ninv": ("sbuf", [128, C], "float32"),
     "us": ("sbuf", [128, C], "bfloat16"),
-    "oinv": ("sbuf", [128, HALF], "float32"),
-    "ysb": ("sbuf", [128, HALF], "bfloat16"),
+    "oinv": ("sbuf", [C, 3 * C], "float32"),
+    "ysb": ("sbuf", [C, 3 * C], "bfloat16"),
     "ps_own": ("psum", [128, 512], "float32"),
-    "ps_ss": ("psum", [128, 512], "float32"),
     "ps_g": ("psum", [128, 512], "float32"),
 }
-SEMAPHORES = ["loaded", "sent", "arr", "c_ones", "s_sq", "t_own", "s_rt", "v_inv", "v_u",
-              "sq_o", "t_ss", "t_g", "s_rto", "v_oinv", "v_y", "stored"]
+SEMAPHORES = ["loaded", "sent", "arr_x", "arr_r", "c_ones", "s_sq", "t_own", "v_rf", "v_rs", "s_rt", "v_u",
+              "t_g", "s_rto", "v_y", "stored"]
 
 
 def _engines(allowed, used, n):
@@ -30,22 +30,6 @@ def _engines(allowed, used, n):
             m |= 1 << b
             n -= 1
     return m
-
-
-def _segments(others):
-    segs = []
-    for h in range(2):
-        c = HALF * h
-        while c < HALF * (h + 1):
-            e = min(HALF * (h + 1), (c // C + 1) * C)
-            y0 = others[c // C] * C + c % C
-            if segs and segs[-1][0] == h and segs[-1][4] == y0:
-                segs[-1][2] = e - HALF * h
-                segs[-1][4] = y0 + e - c
-            else:
-                segs.append([h, c - HALF * h, e - HALF * h, y0, y0 + e - c])
-            c = e
-    return segs
 
 
 def rank_program(g, core, T, topo):
@@ -58,10 +42,7 @@ def rank_program(g, core, T, topo):
     others = [s for s in range(n) if s != rank]
     tens, vec, sca, syn = g.tensor, g.vector, g.scalar, g.sync
 
-    syn.dma_start(T.xs[:], T.x[:]).then_inc(sem.loaded, 16)
-    vec.memset(T.ones[:], 1.0).then_inc(sem.c_ones, 1)
-
-    transfers = []
+    routes = []
     used = 0
     for s in sorted(others, key=lambda s: topo.mask(core, T.cores[s])):
         dst = T.cores[s]
@@ -69,54 +50,56 @@ def rank_program(g, core, T, topo):
         used |= m
         rid, pid, _ = topo.addr(dst)
         slot = rank if rank < s else rank - 1
-        transfers.append(RemoteDMATransfer(dst_ids=[DstId(rid=rid, pnc=pid)], dma_engine_mask=m, remote_sem=sem.arr,
-                                           src=T.xs[:], dst=T.xo[:, slot * C:(slot + 1) * C]))
-    g.wait_ge(sem.loaded, 16)
-    g.remote_dma_fused(transfers, local_sem=sem.sent)
+        routes.append((DstId(rid=rid, pnc=pid), m, slot))
     landed = ENG * len(others)
+
+    def send(src, land, arrival):
+        g.remote_dma_fused([RemoteDMATransfer(dst_ids=[d], dma_engine_mask=m, remote_sem=arrival, src=src,
+                                              dst=land[:, slot * C:(slot + 1) * C]) for d, m, slot in routes],
+                           local_sem=sem.sent)
+
+    syn.dma_start(T.xs[:], T.x[:]).then_inc(sem.loaded, 16)
+    vec.memset(T.ones[:], 1.0).then_inc(sem.c_ones, 1)
+    g.wait_ge(sem.loaded, 16)
+    send(T.xs[:], T.xo, sem.arr_x)
 
     sca.wait_ge(sem.loaded, 16)
     sca.activation(T.sqs[:], T.xs[:], A.Square).then_inc(sem.s_sq, 1)
     tens.wait_ge(sem.c_ones, 1)
     tens.wait_ge(sem.s_sq, 1)
     tens.matmul(T.ps_own[:, 0:C], T.ones[:], T.sqs[:], True, True).then_inc(sem.t_own, 1)
-    sca.wait_ge(sem.t_own, 1)
-    sca.activation(T.ninv[:], T.ps_own[:, 0:C], A.Sqrt).then_inc(sem.s_rt, 1)
+    vec.wait_ge(sem.t_own, 1)
+    vec.reciprocal(T.rf[:], T.ps_own[:, 0:C]).then_inc(sem.v_rf, 1)
+    vec.wait_ge(sem.v_rf, 1)
+    vec.tensor_copy(T.rs[:], T.rf[:]).then_inc(sem.v_rs, 1)
+    g.wait_ge(sem.v_rs, 1)
+    send(T.rs[:], T.ro, sem.arr_r)
+
+    sca.wait_ge(sem.v_rf, 1)
+    sca.activation(T.ninv[:], T.rf[:], A.Sqrt).then_inc(sem.s_rt, 1)
     vec.wait_ge(sem.s_rt, 1)
-    vec.reciprocal(T.ninv[:], T.ninv[:]).then_inc(sem.v_inv, 1)
-    vec.wait_ge(sem.v_inv, 1)
     vec.wait_ge(sem.loaded, 16)
     vec.tensor_tensor(T.us[:], T.xs[:], T.ninv[:], AluOpType.mult).then_inc(sem.v_u, 1)
 
-    sca.wait_ge(sem.arr, landed)
-    sca.activation(T.sqo[:, 0:2 * C], T.xo[:, 0:2 * C], A.Square).then_inc(sem.sq_o, 1)
-    vec.wait_ge(sem.arr, landed)
-    vec.tensor_tensor(T.sqo[:, 2 * C:3 * C], T.xo[:, 2 * C:3 * C], T.xo[:, 2 * C:3 * C],
-                      AluOpType.mult).then_inc(sem.sq_o, 1)
-
-    tens.wait_ge(sem.sq_o, 2)
-    for h in range(2):
-        tens.matmul(T.ps_ss[C * h:C * (h + 1), 0:HALF], T.ones[:, 0:C], T.sqo[:, HALF * h:HALF * (h + 1)],
-                    True, True).then_inc(sem.t_ss, 1)
     tens.wait_ge(sem.v_u, 1)
-    tens.wait_ge(sem.arr, landed)
-    for h in range(2):
-        tens.matmul(T.ps_g[C * h:C * (h + 1), 0:HALF], T.us[:], T.xo[:, HALF * h:HALF * (h + 1)],
-                    True, True).then_inc(sem.t_g, 1)
-
-    sca.wait_ge(sem.t_ss, 2)
-    sca.activation(T.oinv[:], T.ps_ss[:, 0:HALF], A.Sqrt).then_inc(sem.s_rto, 1)
+    tens.wait_ge(sem.arr_x, landed)
+    tens.matmul(T.ps_g[0:C, 0:3 * C], T.us[:], T.xo[:], True, True).then_inc(sem.t_g, 1)
+    sca.wait_ge(sem.arr_r, landed)
+    sca.activation(T.oinv[:], T.ro[0:C, :], A.Sqrt).then_inc(sem.s_rto, 1)
     vec.wait_ge(sem.s_rto, 1)
-    vec.reciprocal(T.oinv[:], T.oinv[:]).then_inc(sem.v_oinv, 1)
-    vec.wait_ge(sem.v_oinv, 1)
-    vec.wait_ge(sem.t_g, 2)
-    vec.tensor_tensor(T.ysb[:], T.ps_g[:, 0:HALF], T.oinv[:], AluOpType.mult).then_inc(sem.v_y, 1)
+    vec.wait_ge(sem.t_g, 1)
+    vec.tensor_tensor(T.ysb[:], T.ps_g[0:C, 0:3 * C], T.oinv[:], AluOpType.mult).then_inc(sem.v_y, 1)
 
-    segs = _segments(others)
+    runs = []
+    for k, s in enumerate(others):
+        if runs and others[k - 1] + 1 == s:
+            runs[-1][1] = k + 1
+        else:
+            runs.append([k, k + 1, s * C])
     syn.wait_ge(sem.v_y, 1)
     sca.wait_ge(sem.v_y, 1)
-    for k, (h, c0, c1, y0, y1) in enumerate(segs):
+    for k, (a, b, y0) in enumerate(runs):
         q = syn if k % 2 == 0 else sca
-        q.dma_start(T.y[:, y0:y1], T.ysb[C * h:C * (h + 1), c0:c1]).then_inc(sem.stored, 16)
-    syn.wait_ge(sem.stored, 16 * len(segs))
-    g.wait_ge(sem.sent, landed)
+        q.dma_start(T.y[:, y0:y0 + (b - a) * C], T.ysb[:, a * C:b * C]).then_inc(sem.stored, 16)
+    syn.wait_ge(sem.stored, 16 * len(runs))
+    g.wait_ge(sem.sent, 2 * landed)

@@ -2,25 +2,32 @@ from concourse.bass import DstId, RemoteDMATransfer
 from concourse.mybir import AluOpType, ActivationFunctionType
 
 C = 64
+H = C // 2
 ENG = 4
 
 SCRATCH = {
+    "xd": ("dram", [128, C], "bfloat16"),
     "xs": ("sbuf", [128, C], "bfloat16"),
     "xo": ("sbuf", [128, 3 * C], "bfloat16"),
-    "ro": ("sbuf", [128, 3 * C], "bfloat16"),
+    "ro": ("sbuf", [128, 3 * H], "float32"),
     "ones": ("sbuf", [128, 128], "bfloat16"),
     "sqs": ("sbuf", [128, C], "bfloat16"),
+    "rp": ("sbuf", [128, H], "float32"),
     "rf": ("sbuf", [128, C], "float32"),
-    "rs": ("sbuf", [128, C], "bfloat16"),
-    "ninv": ("sbuf", [128, C], "float32"),
+    "xr": ("sbuf", [128, C], "float32"),
     "us": ("sbuf", [128, C], "bfloat16"),
     "oinv": ("sbuf", [C, 3 * C], "float32"),
-    "ysb": ("sbuf", [C, 3 * C], "bfloat16"),
+    "ysb": ("sbuf", [C, 4 * C], "bfloat16"),
+    "ps_st": ("psum", [128, 512], "float32"),
     "ps_own": ("psum", [128, 512], "float32"),
-    "ps_g": ("psum", [128, 512], "float32"),
+    "ps_nrm": ("psum", [128, 512], "float32"),
+    "ps_g0": ("psum", [128, 512], "float32"),
+    "ps_g1": ("psum", [128, 512], "float32"),
+    "ps_g2": ("psum", [128, 512], "float32"),
 }
-SEMAPHORES = ["loaded", "sent", "arr_x", "arr_r", "c_ones", "s_sq", "t_own", "v_rf", "v_rs", "s_rt", "v_u",
-              "t_g", "s_rto", "v_y", "stored"]
+SEMAPHORES = ["staged", "loaded", "sent", "ax0", "ax1", "ax2", "ar0", "ar1", "ar2", "c_ones", "c_zero", "s_sq", "t_st",
+              "t_own", "t_nrm", "v_rp", "v_rf", "v_xr", "s_rt", "v_u", "tg0", "tg1", "tg2", "sr0", "sr1", "sr2", "v_y",
+              "stored"]
 
 
 def _engines(allowed, used, n):
@@ -51,55 +58,70 @@ def rank_program(g, core, T, topo):
         rid, pid, _ = topo.addr(dst)
         slot = rank if rank < s else rank - 1
         routes.append((DstId(rid=rid, pnc=pid), m, slot))
-    landed = ENG * len(others)
 
-    def send(src, land, arrival):
-        g.remote_dma_fused([RemoteDMATransfer(dst_ids=[d], dma_engine_mask=m, remote_sem=arrival, src=src,
-                                              dst=land[:, slot * C:(slot + 1) * C]) for d, m, slot in routes],
+    def send(src, land, width, arrival):
+        g.remote_dma_fused([RemoteDMATransfer(dst_ids=[d], dma_engine_mask=m, remote_sem=sem[arrival % slot], src=src,
+                                              dst=land[:, slot * width:(slot + 1) * width]) for d, m, slot in routes],
                            local_sem=sem.sent)
 
-    syn.dma_start(T.xs[:], T.x[:]).then_inc(sem.loaded, 16)
+    syn.dma_start(T.xd[:], T.x[:]).then_inc(sem.staged, 16)
+    sca.dma_start(T.xs[:], T.x[:]).then_inc(sem.loaded, 16)
     vec.memset(T.ones[:], 1.0).then_inc(sem.c_ones, 1)
-    g.wait_ge(sem.loaded, 16)
-    send(T.xs[:], T.xo, sem.arr_x)
+    y_lo, y_hi = others[0] * C, (others[-1] + 1) * C
+    bridge = y_lo < rank * C < y_hi
+    if bridge:
+        vec.memset(T.ysb[:, rank * C:(rank + 1) * C], 0.0).then_inc(sem.c_zero, 1)
+    g.wait_ge(sem.staged, 16)
+    send(T.xd[:], T.xo, C, "ax%d")
 
     sca.wait_ge(sem.loaded, 16)
     sca.activation(T.sqs[:], T.xs[:], A.Square).then_inc(sem.s_sq, 1)
     tens.wait_ge(sem.c_ones, 1)
     tens.wait_ge(sem.s_sq, 1)
+    for h in range(2):
+        tens.matmul(T.ps_st[C * h:C * (h + 1), 0:H], T.ones[:, 0:C], T.sqs[:, H * h:H * (h + 1)],
+                    True, True).then_inc(sem.t_st, 1)
+    tens.matmul(T.ps_nrm[:, 0:C], T.ones[:], T.sqs[:], True, True).then_inc(sem.t_nrm, 1)
     tens.matmul(T.ps_own[:, 0:C], T.ones[:], T.sqs[:], True, True).then_inc(sem.t_own, 1)
+
+    vec.wait_ge(sem.t_st, 2)
+    vec.reciprocal(T.rp[:], T.ps_st[:, 0:H]).then_inc(sem.v_rp, 1)
+    g.wait_ge(sem.v_rp, 1)
+    send(T.rp[:], T.ro, H, "ar%d")
+
     vec.wait_ge(sem.t_own, 1)
     vec.reciprocal(T.rf[:], T.ps_own[:, 0:C]).then_inc(sem.v_rf, 1)
     vec.wait_ge(sem.v_rf, 1)
-    vec.tensor_copy(T.rs[:], T.rf[:]).then_inc(sem.v_rs, 1)
-    g.wait_ge(sem.v_rs, 1)
-    send(T.rs[:], T.ro, sem.arr_r)
-
-    sca.wait_ge(sem.v_rf, 1)
-    sca.activation(T.ninv[:], T.rf[:], A.Sqrt).then_inc(sem.s_rt, 1)
-    vec.wait_ge(sem.s_rt, 1)
     vec.wait_ge(sem.loaded, 16)
-    vec.tensor_tensor(T.us[:], T.xs[:], T.ninv[:], AluOpType.mult).then_inc(sem.v_u, 1)
+    vec.tensor_tensor(T.xr[:], T.xs[:], T.rf[:], AluOpType.mult).then_inc(sem.v_xr, 1)
+    sca.wait_ge(sem.t_nrm, 1)
+    sca.activation(T.ps_nrm[:, 0:C], T.ps_nrm[:, 0:C], A.Sqrt).then_inc(sem.s_rt, 1)
+    vec.wait_ge(sem.s_rt, 1)
+    vec.wait_ge(sem.v_xr, 1)
+    vec.tensor_tensor(T.us[:], T.ps_nrm[:, 0:C], T.xr[:], AluOpType.mult).then_inc(sem.v_u, 1)
 
+    def distance(k):
+        src = T.cores[others[k]]
+        return (topo.chip(src) != topo.chip(core), topo.die(src) != topo.die(core))
+
+    order = sorted(range(len(others)), key=distance)
     tens.wait_ge(sem.v_u, 1)
-    tens.wait_ge(sem.arr_x, landed)
-    tens.matmul(T.ps_g[0:C, 0:3 * C], T.us[:], T.xo[:], True, True).then_inc(sem.t_g, 1)
-    sca.wait_ge(sem.arr_r, landed)
-    sca.activation(T.oinv[:], T.ro[0:C, :], A.Sqrt).then_inc(sem.s_rto, 1)
-    vec.wait_ge(sem.s_rto, 1)
-    vec.wait_ge(sem.t_g, 1)
-    vec.tensor_tensor(T.ysb[:], T.ps_g[0:C, 0:3 * C], T.oinv[:], AluOpType.mult).then_inc(sem.v_y, 1)
+    for k in order:
+        cols = slice(k * C, (k + 1) * C)
+        tens.wait_ge(sem["ax%d" % k], ENG)
+        tens.matmul(T["ps_g%d" % k][0:C, 0:C], T.us[:], T.xo[:, cols], True, True).then_inc(sem["tg%d" % k], 1)
+        sca.wait_ge(sem["ar%d" % k], ENG)
+        for h in range(2):
+            sca.activation(T.oinv[:, k * C + h * H:k * C + (h + 1) * H], T.ro[C * h:C * (h + 1), k * H:(k + 1) * H],
+                           A.Sqrt).then_inc(sem["sr%d" % k], 1)
+        vec.wait_ge(sem["tg%d" % k], 1)
+        vec.wait_ge(sem["sr%d" % k], 2)
+        vec.tensor_tensor(T.ysb[:, others[k] * C:(others[k] + 1) * C], T["ps_g%d" % k][0:C, 0:C], T.oinv[:, cols],
+                          AluOpType.mult).then_inc(sem.v_y, 1)
 
-    runs = []
-    for k, s in enumerate(others):
-        if runs and others[k - 1] + 1 == s:
-            runs[-1][1] = k + 1
-        else:
-            runs.append([k, k + 1, s * C])
-    syn.wait_ge(sem.v_y, 1)
-    sca.wait_ge(sem.v_y, 1)
-    for k, (a, b, y0) in enumerate(runs):
-        q = syn if k % 2 == 0 else sca
-        q.dma_start(T.y[:, y0:y0 + (b - a) * C], T.ysb[:, a * C:b * C]).then_inc(sem.stored, 16)
-    syn.wait_ge(sem.stored, 16 * len(runs))
-    g.wait_ge(sem.sent, 2 * landed)
+    if bridge:
+        syn.wait_ge(sem.c_zero, 1)
+    syn.wait_ge(sem.v_y, len(others))
+    syn.dma_start(T.y[:, y_lo:y_hi], T.ysb[:, y_lo:y_hi]).then_inc(sem.stored, 16)
+    syn.wait_ge(sem.stored, 16)
+    g.wait_ge(sem.sent, 2 * ENG * len(others))

from concourse.bass import DstId, RemoteDMATransfer
from concourse.mybir import AluOpType, ActivationFunctionType

C = 64
H = C // 2
ENG = 4

SCRATCH = {
    "xd": ("dram", [128, C], "bfloat16"),
    "xs": ("sbuf", [128, C], "bfloat16"),
    "xo": ("sbuf", [128, 3 * C], "bfloat16"),
    "ro": ("sbuf", [128, 3 * H], "float32"),
    "ones": ("sbuf", [128, 128], "bfloat16"),
    "sqs": ("sbuf", [128, C], "bfloat16"),
    "rp": ("sbuf", [128, H], "float32"),
    "rf": ("sbuf", [128, C], "float32"),
    "xr": ("sbuf", [128, C], "float32"),
    "us": ("sbuf", [128, C], "bfloat16"),
    "oinv": ("sbuf", [C, 3 * C], "float32"),
    "ysb": ("sbuf", [C, 4 * C], "bfloat16"),
    "ps_st": ("psum", [128, 512], "float32"),
    "ps_own": ("psum", [128, 512], "float32"),
    "ps_nrm": ("psum", [128, 512], "float32"),
    "ps_g0": ("psum", [128, 512], "float32"),
    "ps_g1": ("psum", [128, 512], "float32"),
    "ps_g2": ("psum", [128, 512], "float32"),
}
SEMAPHORES = ["staged", "loaded", "sent", "ax0", "ax1", "ax2", "ar0", "ar1", "ar2", "c_ones", "c_zero", "s_sq", "t_st",
              "t_own", "t_nrm", "v_rp", "v_rf", "v_xr", "s_rt", "v_u", "tg0", "tg1", "tg2", "sr0", "sr1", "sr2", "v_y",
              "stored"]


def _engines(allowed, used, n):
    m = 0
    for b in range(16):
        if n and (allowed >> b) & 1 and not (used >> b) & 1:
            m |= 1 << b
            n -= 1
    return m


def rank_program(g, core, T, topo):
    rank = T.rank_of(core)
    if rank is None:
        return
    sem = T.sem
    A = ActivationFunctionType
    n = len(T.cores)
    others = [s for s in range(n) if s != rank]
    tens, vec, sca, syn = g.tensor, g.vector, g.scalar, g.sync

    routes = []
    used = 0
    for s in sorted(others, key=lambda s: topo.mask(core, T.cores[s])):
        dst = T.cores[s]
        m = _engines(topo.mask(core, dst), used, ENG)
        used |= m
        rid, pid, _ = topo.addr(dst)
        slot = rank if rank < s else rank - 1
        routes.append((DstId(rid=rid, pnc=pid), m, slot))

    def send(src, land, width, arrival):
        g.remote_dma_fused([RemoteDMATransfer(dst_ids=[d], dma_engine_mask=m, remote_sem=sem[arrival % slot], src=src,
                                              dst=land[:, slot * width:(slot + 1) * width]) for d, m, slot in routes],
                           local_sem=sem.sent)

    syn.dma_start(T.xd[:], T.x[:]).then_inc(sem.staged, 16)
    sca.dma_start(T.xs[:], T.x[:]).then_inc(sem.loaded, 16)
    vec.memset(T.ones[:], 1.0).then_inc(sem.c_ones, 1)
    y_lo, y_hi = others[0] * C, (others[-1] + 1) * C
    bridge = y_lo < rank * C < y_hi
    if bridge:
        vec.memset(T.ysb[:, rank * C:(rank + 1) * C], 0.0).then_inc(sem.c_zero, 1)
    g.wait_ge(sem.staged, 16)
    send(T.xd[:], T.xo, C, "ax%d")

    sca.wait_ge(sem.loaded, 16)
    sca.activation(T.sqs[:], T.xs[:], A.Square).then_inc(sem.s_sq, 1)
    tens.wait_ge(sem.c_ones, 1)
    tens.wait_ge(sem.s_sq, 1)
    for h in range(2):
        tens.matmul(T.ps_st[C * h:C * (h + 1), 0:H], T.ones[:, 0:C], T.sqs[:, H * h:H * (h + 1)],
                    True, True).then_inc(sem.t_st, 1)
    tens.matmul(T.ps_nrm[:, 0:C], T.ones[:], T.sqs[:], True, True).then_inc(sem.t_nrm, 1)
    tens.matmul(T.ps_own[:, 0:C], T.ones[:], T.sqs[:], True, True).then_inc(sem.t_own, 1)

    vec.wait_ge(sem.t_st, 2)
    vec.reciprocal(T.rp[:], T.ps_st[:, 0:H]).then_inc(sem.v_rp, 1)
    g.wait_ge(sem.v_rp, 1)
    send(T.rp[:], T.ro, H, "ar%d")

    vec.wait_ge(sem.t_own, 1)
    vec.reciprocal(T.rf[:], T.ps_own[:, 0:C]).then_inc(sem.v_rf, 1)
    vec.wait_ge(sem.v_rf, 1)
    vec.wait_ge(sem.loaded, 16)
    vec.tensor_tensor(T.xr[:], T.xs[:], T.rf[:], AluOpType.mult).then_inc(sem.v_xr, 1)
    sca.wait_ge(sem.t_nrm, 1)
    sca.activation(T.ps_nrm[:, 0:C], T.ps_nrm[:, 0:C], A.Sqrt).then_inc(sem.s_rt, 1)
    vec.wait_ge(sem.s_rt, 1)
    vec.wait_ge(sem.v_xr, 1)
    vec.tensor_tensor(T.us[:], T.ps_nrm[:, 0:C], T.xr[:], AluOpType.mult).then_inc(sem.v_u, 1)

    def distance(k):
        src = T.cores[others[k]]
        return (topo.chip(src) != topo.chip(core), topo.die(src) != topo.die(core))

    order = sorted(range(len(others)), key=distance)
    tens.wait_ge(sem.v_u, 1)
    for k in order:
        cols = slice(k * C, (k + 1) * C)
        tens.wait_ge(sem["ax%d" % k], ENG)
        tens.matmul(T["ps_g%d" % k][0:C, 0:C], T.us[:], T.xo[:, cols], True, True).then_inc(sem["tg%d" % k], 1)
        sca.wait_ge(sem["ar%d" % k], ENG)
        for h in range(2):
            sca.activation(T.oinv[:, k * C + h * H:k * C + (h + 1) * H], T.ro[C * h:C * (h + 1), k * H:(k + 1) * H],
                           A.Sqrt).then_inc(sem["sr%d" % k], 1)
        vec.wait_ge(sem["tg%d" % k], 1)
        vec.wait_ge(sem["sr%d" % k], 2)
        vec.tensor_tensor(T.ysb[:, others[k] * C:(others[k] + 1) * C], T["ps_g%d" % k][0:C, 0:C], T.oinv[:, cols],
                          AluOpType.mult).then_inc(sem.v_y, 1)

    if bridge:
        syn.wait_ge(sem.c_zero, 1)
    syn.wait_ge(sem.v_y, len(others))
    syn.dma_start(T.y[:, y_lo:y_hi], T.ysb[:, y_lo:y_hi]).then_inc(sem.stored, 16)
    syn.wait_ge(sem.stored, 16)
    g.wait_ge(sem.sent, 2 * ENG * len(others))
